import numpy as np, ml_dtypes
CORES = [34,162,290,418,42,426]
N = 6
import mx_ref
NC = 256
BF = ml_dtypes.bfloat16
def setup_inputs(rng):
    def f(*shape):
        return mx_ref.flush((rng.standard_normal(shape, dtype=np.float32) * np.exp2(rng.integers(-2, 3, shape[:-1] + (1,)))).astype(BF))
    return {"x": f(N, 128, 512), "rt": f(N, 128, 512), "w": f(N, 128, 4 * NC)}
def setup_inputs_blocks(rng):
    d = setup_inputs(rng)
    for k in ("x", "rt", "w"): d[k] = mx_ref.spread(d[k], rng, 1)
    return d
def setup_inputs_wide(rng):
    d = setup_inputs(rng)
    for k in ("x", "rt", "w"): d[k] = mx_ref.flush((d[k].astype(np.float32) * np.exp2(rng.integers(-6, 7, (N, 1, 1))).astype(np.float32)).astype(BF))
    return d
def setup_inputs_near(rng):
    d = setup_inputs(rng); v = d["rt"].astype(np.float32).reshape(N, 128, -1, 4)
    d["rt"] = mx_ref.flush((v[:, :, :1] + v / 64).reshape(d["rt"].shape).astype(BF))
    return d
def setup_inputs_twins(rng):
    d = setup_inputs(rng); v = d["rt"].reshape(N, 128, -1, 4).copy()
    v[:, :, 1] = v[:, :, 0]
    d["rt"] = v.reshape(d["rt"].shape)
    return d
def reference(x, rt, w):
    W = [mx_ref.quantize(w[e]) for e in range(N)]
    y = np.zeros((N, 128, NC), np.float32)
    for j in range(N):
        X = mx_ref.quantize(x[j])
        lg = mx_ref.matmul(X, mx_ref.quantize(rt[j]))[:, :N]
        m = lg.max(axis=1, keepdims=True); m2 = np.where(lg < m, lg, -np.inf).max(axis=1, keepdims=True)
        for e in range(N):
            y[j] = y[j] + (lg[:, e:e + 1] >= m2) * (mx_ref.matmul(X, W[e]) * lg[:, e:e + 1])
    return {"y": y}

@@ -1,0 +1,178 @@
+from concourse.bass import DstId, RemoteDMATransfer
+from concourse.mybir import dt, AluOpType, AxisListType, ActivationFunctionType
+
+N = 6
+NC = 256
+NT = 128
+BANK = 512
+FAR = -1e29
+
+SCRATCH = {
+    "wt": ("sbuf", [128, 4 * NC], "bfloat16"),
+    "xt": ("sbuf", [128, 4 * NT], "bfloat16"),
+    "rtt": ("sbuf", [128, 512], "bfloat16"),
+    "wc": ("sbuf", [128, N * NC], "float8_e4m3fn_x4"),
+    "ws": ("sbuf", [128, N * NC], "uint8"),
+    "xc": ("sbuf", [128, NT], "float8_e4m3fn_x4"),
+    "xs": ("sbuf", [128, NT], "uint8"),
+    "rc": ("sbuf", [128, 128], "float8_e4m3fn_x4"),
+    "rs": ("sbuf", [128, 128], "uint8"),
+    "m1": ("sbuf", [128, 4], "float32"),
+    "m2": ("sbuf", [128, 4], "float32"),
+    "ta": ("sbuf", [128, 8], "float32"),
+    "tb": ("sbuf", [128, 8], "float32"),
+    "tc": ("sbuf", [128, 8], "float32"),
+    "gate": ("sbuf", [128, 8], "float32"),
+    "z": ("sbuf", [128, N * NC], "float32"),
+    "acc": ("sbuf", [128, NC], "float32"),
+    "ps": ("psum", [128, 8 * BANK], "float32"),
+}
+SEMAPHORES = (["lw", "lx", "lr", "qw", "qx", "mm", "rv", "gt", "zs", "av", "st", "sent",
+               "pin", "cin", "hin", "cnext", "chelp", "cprev"] + ["pl%d" % r for r in range(N)])
+
+
+def plan(cores, topo):
+    n = len(cores)
+    rk = [topo.rack(topo.host(c)) for c in cores]
+    partner = {}
+    for r, c in enumerate(cores):
+        partner[r] = [s for s, d in enumerate(cores) if rk[s] != rk[r] and topo.chip(d) == topo.chip(c)
+                      and topo.may_write(c, d)][0]
+    nxt, prv = {}, {}
+    for rack in sorted(set(rk)):
+        ring = sorted([r for r in range(n) if rk[r] == rack], key=lambda r: min(r, partner[r]))
+        for i, r in enumerate(ring):
+            nxt[r], prv[r] = ring[(i + 1) % len(ring)], ring[i - 1]
+    order = []
+    for r in range(n):
+        if r not in order:
+            order += [r, partner[r]]
+    slot = {r: order.index(r) for r in range(n)}
+    base = {r: min(slot[r], slot[partner[r]]) for r in range(n)}
+    helper = {}
+    for r, c in enumerate(cores):
+        first = c - c % 8
+        helper[r] = [h for h in range(first, first + 8) if topo.die(h) != topo.die(c)
+                     and topo.may_write(h, cores[prv[r]])][0]
+    return partner, nxt, prv, slot, base, helper
+
+
+def rank_program(g, core, T, topo):
+    cores = list(T.cores)
+    partner, nxt, prv, slot, base, helper = plan(cores, topo)
+    S = T.sem
+
+    def codes(a, k=1):
+        return T.wc[:, a * NC:(a + k) * NC].bitcast(dt.uint8)
+
+    def planes(a, k=1):
+        return T.ws[:, a * NC:(a + k) * NC]
+
+    def send(dsts, view, sem, mask):
+        ids = []
+        for d in dsts:
+            rid, pid = topo.addr(d, core)
+            ids.append(DstId(rid=rid, pnc=pid))
+        return RemoteDMATransfer(dst_ids=ids, dma_engine_mask=mask, remote_sem=sem, srcs=[view], dsts=[view] * len(ids))
+
+    rank = T.rank_of(core)
+    if rank is None:
+        for r in range(N):
+            if helper[r] == core:
+                d = cores[prv[r]]
+                m = topo.mask(core, d)
+                g.wait_ge(S.hin, bin(topo.mask(cores[r], core) & ~topo.mask(cores[r], cores[partner[r]])).count("1"))
+                g.remote_dma_fused([send([d], codes(slot[r]), S.chelp, m)], local_sem=S.sent)
+                g.wait_ge(S.sent, bin(m).count("1"))
+        return
+
+    pa, cn, cp, hp = cores[partner[rank]], cores[nxt[rank]], cores[prv[rank]], helper[rank]
+    mpa, mn, mp = topo.mask(core, pa), topo.mask(core, cn), topo.mask(core, cp)
+    mhp = topo.mask(core, hp) & ~mpa
+    both = mn & mp
+    ne = bin(mpa).count("1")
+    cnt = lambda m: bin(m).count("1")
+    me, po = slot[rank], slot[partner[rank]]
+
+    g.sync.dma_start(T.wt[:], T.w[:]).then_inc(S.lw, 16)
+    g.sync.dma_start(T.xt[:], T.x[:]).then_inc(S.lx, 16)
+    g.sync.dma_start(T.rtt[:], T.rt[:]).then_inc(S.lr, 16)
+
+    g.wait_ge(S.qw, 1)
+    g.remote_dma_fused([send([pa], planes(me), S.pin, mpa)], local_sem=S.sent)
+    g.remote_dma_fused([send([pa], codes(me), S.cin, mpa), send([hp], codes(me), S.hin, mhp)], local_sem=S.sent)
+    g.wait_ge(S.pin, ne)
+    g.remote_dma_fused([send([cn, cp], planes(base[rank], 2), S["pl%d" % rank], both)], local_sem=S.sent)
+    g.wait_ge(S.cin, ne)
+    g.remote_dma_fused([send([cn], codes(base[rank], 2), S.cnext, mn)], local_sem=S.sent)
+    g.remote_dma_fused([send([cp], codes(po), S.cprev, mp)], local_sem=S.sent)
+    g.wait_ge(S.sent, 2 * cnt(mpa) + cnt(mhp) + cnt(both) + cnt(mn) + cnt(mp))
+
+    up, dn = prv[rank], nxt[rank]
+    full = cnt(both)
+    tiles = [
+        (rank, []),
+        (partner[rank], [(S.pin, ne), (S.cin, ne)]),
+        (up, [(S["pl%d" % up], full), (S.cnext, ne)]),
+        (partner[up], []),
+        (dn, [(S["pl%d" % dn], full), (S.chelp, ne)]),
+        (partner[dn], [(S.cprev, ne)]),
+    ]
+
+    v = g.vector
+    v.wait_ge(S.lw, 16)
+    v.quantize_mx(T.wc[:, me * NC:(me + 1) * NC], T.ws[:, me * NC:(me + 1) * NC], T.wt[:]).then_inc(S.qw, 1)
+    v.wait_ge(S.lx, 16)
+    v.quantize_mx(T.xc[:], T.xs[:], T.xt[:]).then_inc(S.qx, 1)
+    v.wait_ge(S.lr, 16)
+    v.quantize_mx(T.rc[:], T.rs[:], T.rtt[:]).then_inc(S.qx, 1)
+
+    t = g.tensor
+    t.wait_ge(S.qx, 2)
+    t.matmul_mx(T.ps[:, 0:128], T.xc[:], T.xs[:], T.rc[:], T.rs[:], True, True).then_inc(S.mm, 1)
+    t.wait_ge(S.qw, 1)
+    parts = []
+    for i, (e, waits) in enumerate(tiles):
+        for s, n in waits:
+            t.wait_ge(s, n)
+        pieces = [(0, NC)] if i + 1 < N else [(0, NC // 2), (NC // 2, NC // 2)]
+        for c0, w in pieces:
+            b = 1 + len(parts)
+            a = slot[e] * NC + c0
+            t.matmul_mx(T.ps[:, b * BANK:b * BANK + w], T.xc[:], T.xs[:], T.wc[:, a:a + w], T.ws[:, a:a + w],
+                        True, True).then_inc(S.mm, 1)
+            parts.append((e, c0, w, b, i))
+
+    L = T.ps[:, 0:N]
+    v.wait_ge(S.mm, 1)
+    v.tensor_reduce(T.m1[:, 0:1], L, AxisListType.X, AluOpType.max).then_inc(S.rv, 1)
+    v.wait_ge(S.rv, 1)
+    v.tensor_scalar(T.ta[:, 0:N], L, T.m1[:, 0:1], FAR, AluOpType.is_ge, AluOpType.mult).then_inc(S.rv, 1)
+    v.wait_ge(S.rv, 2)
+    v.tensor_tensor(T.tb[:, 0:N], L, T.ta[:, 0:N], AluOpType.add).then_inc(S.rv, 1)
+    v.wait_ge(S.rv, 3)
+    v.tensor_reduce(T.m2[:, 0:1], T.tb[:, 0:N], AxisListType.X, AluOpType.max).then_inc(S.rv, 1)
+    v.wait_ge(S.rv, 4)
+    v.tensor_scalar(T.tc[:, 0:N], L, T.m2[:, 0:1], None, AluOpType.is_ge).then_inc(S.rv, 1)
+    v.wait_ge(S.rv, 5)
+    v.tensor_tensor(T.gate[:, 0:N], L, T.tc[:, 0:N], AluOpType.mult).then_inc(S.gt, 1)
+
+    g.scalar.wait_ge(S.gt, 1)
+    for k, (e, c0, w, b, i) in enumerate(parts):
+        g.scalar.wait_ge(S.mm, 2 + k)
+        g.scalar.activation(T.z[:, i * NC + c0:i * NC + c0 + w], T.ps[:, b * BANK:b * BANK + w],
+                            ActivationFunctionType.Copy, scale=T.gate[:, e:e + 1]).then_inc(S.zs, 1)
+
+    done = 0
+    for k, (e, c0, w, b, i) in enumerate(parts):
+        if i == 0:
+            continue
+        v.wait_ge(S.zs, k + 1)
+        if done and (i + 1 < N or c0 == 0):
+            v.wait_ge(S.av, done)
+        prev = T.z[:, c0:c0 + w] if i == 1 else T.acc[:, c0:c0 + w]
+        v.tensor_tensor(T.acc[:, c0:c0 + w], prev, T.z[:, i * NC + c0:i * NC + c0 + w], AluOpType.add).then_inc(S.av, 1)
+        done += 1
+    g.sync.wait_ge(S.av, done)
+    g.sync.dma_start(T.y[:], T.acc[:]).then_inc(S.st, 16)
+    g.sync.wait_ge(S.st, 16)

@@ -28,7 +28,7 @@ SCRATCH = {
     "ps": ("psum", [128, 8 * BANK], "float32"),
 }
 SEMAPHORES = (["lw", "lx", "lr", "qw", "qx", "mm", "rv", "gt", "zs", "av", "st", "sent",
-               "pin", "cin", "hin", "cnext", "chelp", "cprev"] + ["pl%d" % r for r in range(N)])
+               "pin", "cin", "hin", "rnext", "rprev", "onext", "oprev"] + ["pl%d" % r for r in range(N)])
 
 
 def plan(cores, topo):
@@ -53,7 +53,7 @@ def plan(cores, topo):
     for r, c in enumerate(cores):
         first = c - c % 8
         helper[r] = [h for h in range(first, first + 8) if topo.die(h) != topo.die(c)
-                     and topo.may_write(h, cores[prv[r]])][0]
+                     and topo.may_write(h, cores[prv[r]]) and topo.may_write(h, cores[nxt[r]])][0]
     return partner, nxt, prv, slot, base, helper
 
 
@@ -61,6 +61,9 @@ def rank_program(g, core, T, topo):
     cores = list(T.cores)
     partner, nxt, prv, slot, base, helper = plan(cores, topo)
     S = T.sem
+
+    def cnt(m):
+        return bin(m).count("1")
 
     def codes(a, k=1):
         return T.wc[:, a * NC:(a + k) * NC].bitcast(dt.uint8)
@@ -79,19 +82,19 @@ def rank_program(g, core, T, topo):
     if rank is None:
         for r in range(N):
             if helper[r] == core:
-                d = cores[prv[r]]
-                m = topo.mask(core, d)
-                g.wait_ge(S.hin, bin(topo.mask(cores[r], core) & ~topo.mask(cores[r], cores[partner[r]])).count("1"))
-                g.remote_dma_fused([send([d], codes(slot[r]), S.chelp, m)], local_sem=S.sent)
-                g.wait_ge(S.sent, bin(m).count("1"))
+                d, f = cores[prv[r]], cores[nxt[r]]
+                m = topo.mask(core, d) & topo.mask(core, f)
+                g.wait_ge(S.hin, cnt(topo.mask(cores[r], core) & ~topo.mask(cores[r], cores[partner[r]])))
+                g.remote_dma_fused([send([d], codes(slot[r]), S.oprev, m)], local_sem=S.sent)
+                g.remote_dma_fused([send([f], codes(slot[r]), S.onext, m)], local_sem=S.sent)
+                g.wait_ge(S.sent, 2 * cnt(m))
         return
 
     pa, cn, cp, hp = cores[partner[rank]], cores[nxt[rank]], cores[prv[rank]], helper[rank]
     mpa, mn, mp = topo.mask(core, pa), topo.mask(core, cn), topo.mask(core, cp)
     mhp = topo.mask(core, hp) & ~mpa
     both = mn & mp
-    ne = bin(mpa).count("1")
-    cnt = lambda m: bin(m).count("1")
+    ne = cnt(mpa)
     me, po = slot[rank], slot[partner[rank]]
 
     g.sync.dma_start(T.wt[:], T.w[:]).then_inc(S.lw, 16)
@@ -104,8 +107,8 @@ def rank_program(g, core, T, topo):
     g.wait_ge(S.pin, ne)
     g.remote_dma_fused([send([cn, cp], planes(base[rank], 2), S["pl%d" % rank], both)], local_sem=S.sent)
     g.wait_ge(S.cin, ne)
-    g.remote_dma_fused([send([cn], codes(base[rank], 2), S.cnext, mn)], local_sem=S.sent)
-    g.remote_dma_fused([send([cp], codes(po), S.cprev, mp)], local_sem=S.sent)
+    g.remote_dma_fused([send([cn], codes(po), S.rnext, mn)], local_sem=S.sent)
+    g.remote_dma_fused([send([cp], codes(po), S.rprev, mp)], local_sem=S.sent)
     g.wait_ge(S.sent, 2 * cnt(mpa) + cnt(mhp) + cnt(both) + cnt(mn) + cnt(mp))
 
     up, dn = prv[rank], nxt[rank]
@@ -113,10 +116,10 @@ def rank_program(g, core, T, topo):
     tiles = [
         (rank, []),
         (partner[rank], [(S.pin, ne), (S.cin, ne)]),
-        (up, [(S["pl%d" % up], full), (S.cnext, ne)]),
-        (partner[up], []),
-        (dn, [(S["pl%d" % dn], full), (S.chelp, ne)]),
-        (partner[dn], [(S.cprev, ne)]),
+        (partner[up], [(S["pl%d" % up], full), (S.rnext, ne)]),
+        (dn, [(S["pl%d" % dn], full), (S.oprev, ne)]),
+        (partner[dn], [(S.rprev, ne)]),
+        (up, [(S.onext, ne)]),
     ]
 
     v = g.vector

@@ -3,6 +3,7 @@ from concourse.mybir import dt, AluOpType, AxisListType, ActivationFunctionType
 
 N = 6
 NC = 256
+NB = 160
 NT = 128
 BANK = 512
 FAR = -1e29
@@ -27,8 +28,9 @@ SCRATCH = {
     "acc": ("sbuf", [128, NC], "float32"),
     "ps": ("psum", [128, 8 * BANK], "float32"),
 }
-SEMAPHORES = (["lw", "lx", "lr", "qw", "qx", "mm", "rv", "gt", "zs", "av", "st", "sent",
-               "pin", "cin", "hin", "rnext", "rprev", "onext", "oprev"] + ["pl%d" % r for r in range(N)])
+SEMAPHORES = (["lw", "lx", "lr", "qw", "qx", "mm", "rv", "gt", "zs", "av", "st", "sent", "pin", "ain", "bin", "hin",
+               "rnextA", "rprevA", "onextA", "oprevA", "rnextB", "rprevB", "onextB", "oprevB"]
+              + ["pl%d" % r for r in range(N)])
 
 
 def plan(cores, topo):
@@ -49,24 +51,27 @@ def plan(cores, topo):
             order += [r, partner[r]]
     slot = {r: order.index(r) for r in range(n)}
     base = {r: min(slot[r], slot[partner[r]]) for r in range(n)}
-    helper = {}
+    gatec, helpB, helpA = {}, {}, {}
     for r, c in enumerate(cores):
         first = c - c % 8
-        helper[r] = [h for h in range(first, first + 8) if topo.die(h) != topo.die(c)
-                     and topo.may_write(h, cores[prv[r]]) and topo.may_write(h, cores[nxt[r]])][0]
-    return partner, nxt, prv, slot, base, helper
+        near = [h for h in range(first, first + 8) if h != c
+                and topo.may_write(h, cores[prv[r]]) and topo.may_write(h, cores[nxt[r]])]
+        near.sort(key=lambda h: topo.die(h) != topo.die(c))
+        gatec[r], helpB[r], helpA[r] = near[0], near[-2], near[-1]
+    return partner, nxt, prv, slot, base, gatec, helpB, helpA
 
 
 def rank_program(g, core, T, topo):
     cores = list(T.cores)
-    partner, nxt, prv, slot, base, helper = plan(cores, topo)
+    partner, nxt, prv, slot, base, gatec, helpB, helpA = plan(cores, topo)
     S = T.sem
 
     def cnt(m):
         return bin(m).count("1")
 
-    def codes(a, k=1):
-        return T.wc[:, a * NC:(a + k) * NC].bitcast(dt.uint8)
+    def codes(a, run):
+        c0, c1 = (0, NB) if run == "B" else (NB, NC)
+        return T.wc[:, a * NC + c0:a * NC + c1].bitcast(dt.uint8)
 
     def planes(a, k=1):
         return T.ws[:, a * NC:(a + k) * NC]
@@ -78,24 +83,38 @@ def rank_program(g, core, T, topo):
             ids.append(DstId(rid=rid, pnc=pid))
         return RemoteDMATransfer(dst_ids=ids, dma_engine_mask=mask, remote_sem=sem, srcs=[view], dsts=[view] * len(ids))
 
+    def onchip(src, dst, far):
+        return topo.mask(src, dst) & ~topo.mask(src, far)
+
     rank = T.rank_of(core)
     if rank is None:
         for r in range(N):
-            if helper[r] == core:
-                d, f = cores[prv[r]], cores[nxt[r]]
-                m = topo.mask(core, d) & topo.mask(core, f)
-                g.wait_ge(S.hin, cnt(topo.mask(cores[r], core) & ~topo.mask(cores[r], cores[partner[r]])))
-                g.remote_dma_fused([send([d], codes(slot[r]), S.oprev, m)], local_sem=S.sent)
-                g.remote_dma_fused([send([f], codes(slot[r]), S.onext, m)], local_sem=S.sent)
-                g.wait_ge(S.sent, 2 * cnt(m))
+            cr, cn, cp = cores[r], cores[nxt[r]], cores[prv[r]]
+            if core == gatec[r]:
+                a, pa = slot[partner[r]], cores[partner[r]]
+                mn, mp, mr = topo.mask(core, cn), topo.mask(core, cp), onchip(core, cr, cn)
+                g.wait_ge(S.hin, cnt(topo.mask(pa, core)))
+                g.remote_dma_fused([send([cn], codes(a, "B"), S.rnextB, mn)], local_sem=S.sent)
+                g.remote_dma_fused([send([cp], codes(a, "B"), S.rprevB, mp)], local_sem=S.sent)
+                g.remote_dma_fused([send([cr], codes(a, "B"), S.bin, mr)], local_sem=S.sent)
+                g.wait_ge(S.sent, cnt(mn) + cnt(mp) + cnt(mr))
+            for run, h in (("B", helpB[r]), ("A", helpA[r])):
+                if core == h:
+                    a = slot[r]
+                    mn, mp = topo.mask(core, cn), topo.mask(core, cp)
+                    g.wait_ge(S.hin, cnt(onchip(cr, core, cores[partner[r]])))
+                    g.remote_dma_fused([send([cp], codes(a, run), S["oprev" + run], mp)], local_sem=S.sent)
+                    g.remote_dma_fused([send([cn], codes(a, run), S["onext" + run], mn)], local_sem=S.sent)
+                    g.wait_ge(S.sent, cnt(mn) + cnt(mp))
         return
 
-    pa, cn, cp, hp = cores[partner[rank]], cores[nxt[rank]], cores[prv[rank]], helper[rank]
-    mpa, mn, mp = topo.mask(core, pa), topo.mask(core, cn), topo.mask(core, cp)
-    mhp = topo.mask(core, hp) & ~mpa
+    pr = partner[rank]
+    pa, pg, cn, cp = cores[pr], gatec[pr], cores[nxt[rank]], cores[prv[rank]]
+    hb, ha = helpB[rank], helpA[rank]
+    mpa, mpg, mn, mp = topo.mask(core, pa), topo.mask(core, pg), topo.mask(core, cn), topo.mask(core, cp)
+    mhb, mha = onchip(core, hb, pg), onchip(core, ha, pa)
     both = mn & mp
-    ne = cnt(mpa)
-    me, po = slot[rank], slot[partner[rank]]
+    me, po = slot[rank], slot[pr]
 
     g.sync.dma_start(T.wt[:], T.w[:]).then_inc(S.lw, 16)
     g.sync.dma_start(T.xt[:], T.x[:]).then_inc(S.lx, 16)
@@ -103,23 +122,27 @@ def rank_program(g, core, T, topo):
 
     g.wait_ge(S.qw, 1)
     g.remote_dma_fused([send([pa], planes(me), S.pin, mpa)], local_sem=S.sent)
-    g.remote_dma_fused([send([pa], codes(me), S.cin, mpa), send([hp], codes(me), S.hin, mhp)], local_sem=S.sent)
-    g.wait_ge(S.pin, ne)
+    g.remote_dma_fused([send([pg], codes(me, "B"), S.hin, mpg), send([hb], codes(me, "B"), S.hin, mhb)], local_sem=S.sent)
+    g.remote_dma_fused([send([pa], codes(me, "A"), S.ain, mpa), send([ha], codes(me, "A"), S.hin, mha)], local_sem=S.sent)
+    g.wait_ge(S.pin, cnt(topo.mask(pa, core)))
     g.remote_dma_fused([send([cn, cp], planes(base[rank], 2), S["pl%d" % rank], both)], local_sem=S.sent)
-    g.wait_ge(S.cin, ne)
-    g.remote_dma_fused([send([cn], codes(po), S.rnext, mn)], local_sem=S.sent)
-    g.remote_dma_fused([send([cp], codes(po), S.rprev, mp)], local_sem=S.sent)
-    g.wait_ge(S.sent, 2 * cnt(mpa) + cnt(mhp) + cnt(both) + cnt(mn) + cnt(mp))
+    g.wait_ge(S.ain, cnt(topo.mask(pa, core)))
+    g.remote_dma_fused([send([cn], codes(po, "A"), S.rnextA, mn)], local_sem=S.sent)
+    g.remote_dma_fused([send([cp], codes(po, "A"), S.rprevA, mp)], local_sem=S.sent)
+    g.wait_ge(S.sent, 2 * cnt(mpa) + cnt(mpg) + cnt(mhb) + cnt(mha) + cnt(both) + cnt(mn) + cnt(mp))
 
     up, dn = prv[rank], nxt[rank]
-    full = cnt(both)
+    cu, cd = cores[up], cores[dn]
+    pu = cnt(topo.mask(cu, core) & topo.mask(cu, cores[prv[up]]))
+    pd = cnt(topo.mask(cd, core) & topo.mask(cd, cores[nxt[dn]]))
     tiles = [
         (rank, []),
-        (partner[rank], [(S.pin, ne), (S.cin, ne)]),
-        (partner[up], [(S["pl%d" % up], full), (S.rnext, ne)]),
-        (dn, [(S["pl%d" % dn], full), (S.oprev, ne)]),
-        (partner[dn], [(S.rprev, ne)]),
-        (up, [(S.onext, ne)]),
+        (pr, [(S.pin, cnt(topo.mask(pa, core))), (S.ain, cnt(topo.mask(pa, core))),
+              (S.bin, cnt(onchip(gatec[rank], core, cn)))]),
+        (dn, [(S["pl%d" % dn], pd), (S.oprevB, cnt(topo.mask(helpB[dn], core))), (S.oprevA, cnt(topo.mask(helpA[dn], core)))]),
+        (partner[up], [(S["pl%d" % up], pu), (S.rnextB, cnt(topo.mask(gatec[up], core))), (S.rnextA, cnt(topo.mask(cu, core)))]),
+        (up, [(S.onextB, cnt(topo.mask(helpB[up], core))), (S.onextA, cnt(topo.mask(helpA[up], core)))]),
+        (partner[dn], [(S.rprevB, cnt(topo.mask(gatec[dn], core))), (S.rprevA, cnt(topo.mask(cd, core)))]),
     ]
 
     v = g.vector

@@ -3,10 +3,19 @@ from concourse.mybir import dt, AluOpType, AxisListType, ActivationFunctionType
 
 N = 6
 NC = 256
-NB = 160
+NH = 128
 NT = 128
 BANK = 512
 FAR = -1e29
+
+SCHED = {
+    "R": [("own", "0", ["pK"]), ("own", "s", ["pR"]), ("own", "0", ["G"]), ("own", "1", ["pR"]), ("own", "1", ["H"]),
+          ("own", "S", ["p", "n"]), ("par", "1", ["n"]), ("par", "1", ["p"])],
+    "G": [("own", "0", ["p"]), ("own", "0", ["n"])],
+    "H": [("own", "1", ["p"]), ("own", "1", ["n"])],
+    "K": [("par", "0", ["n"]), ("par", "0", ["p"]), ("par", "0", ["R"])],
+}
+ORDER = [("own", False), ("par", False), ("nx", True), ("pvpar", True), ("pv", True), ("nxpar", True)]
 
 SCRATCH = {
     "wt": ("sbuf", [128, 4 * NC], "bfloat16"),
@@ -28,19 +37,17 @@ SCRATCH = {
     "acc": ("sbuf", [128, NC], "float32"),
     "ps": ("psum", [128, 8 * BANK], "float32"),
 }
-SEMAPHORES = (["lw", "lx", "lr", "qw", "qx", "mm", "rv", "gt", "zs", "av", "st", "sent", "pin", "ain", "bin", "hin",
-               "rnextA", "rprevA", "onextA", "oprevA", "rnextB", "rprevB", "onextB", "oprevB"]
-              + ["pl%d" % r for r in range(N)])
+SEMAPHORES = (["lw0", "lw1", "lx", "lr", "qw0", "qw1", "qx", "mm", "rv", "gt", "zs", "av", "st0", "st1", "sent"]
+              + ["a%d%s" % (e, p) for e in range(N) for p in "01sS"])
 
 
 def plan(cores, topo):
     n = len(cores)
     rk = [topo.rack(topo.host(c)) for c in cores]
-    partner = {}
+    partner, nxt, prv = {}, {}, {}
     for r, c in enumerate(cores):
         partner[r] = [s for s, d in enumerate(cores) if rk[s] != rk[r] and topo.chip(d) == topo.chip(c)
                       and topo.may_write(c, d)][0]
-    nxt, prv = {}, {}
     for rack in sorted(set(rk)):
         ring = sorted([r for r in range(n) if rk[r] == rack], key=lambda r: min(r, partner[r]))
         for i, r in enumerate(ring):
@@ -50,120 +57,120 @@ def plan(cores, topo):
         if r not in order:
             order += [r, partner[r]]
     slot = {r: order.index(r) for r in range(n)}
-    base = {r: min(slot[r], slot[partner[r]]) for r in range(n)}
-    gatec, helpB, helpA = {}, {}, {}
+    role = {}
     for r, c in enumerate(cores):
         first = c - c % 8
         near = [h for h in range(first, first + 8) if h != c
                 and topo.may_write(h, cores[prv[r]]) and topo.may_write(h, cores[nxt[r]])]
         near.sort(key=lambda h: topo.die(h) != topo.die(c))
-        gatec[r], helpB[r], helpA[r] = near[0], near[-2], near[-1]
-    return partner, nxt, prv, slot, base, gatec, helpB, helpA
+        role[r] = {"R": c, "G": near[0], "H": near[-2], "K": near[-1]}
+    return partner, nxt, prv, slot, role
+
+
+def calls(cores, topo):
+    partner, nxt, prv, slot, role = plan(cores, topo)
+    out, lands = {}, {}
+    for r in range(len(cores)):
+        tile = {"own": r, "par": partner[r]}
+        place = dict(role[r])
+        place.update({"n": cores[nxt[r]], "p": cores[prv[r]]})
+        for k, c in role[partner[r]].items():
+            place["p" + k] = c
+        for k, rows in SCHED.items():
+            src = role[r][k]
+            for t, piece, dst in rows:
+                ds = [place[d] for d in dst]
+                m = topo.mask(src, ds[0])
+                for d in ds[1:]:
+                    m &= topo.mask(src, d)
+                if dst[0] in role[r]:
+                    m &= ~topo.mask(src, place["n"])
+                out.setdefault(src, []).append((tile[t], piece, ds, m))
+                for d in ds:
+                    lands[d, tile[t], piece] = bin(m).count("1")
+    return out, lands
 
 
 def rank_program(g, core, T, topo):
     cores = list(T.cores)
-    partner, nxt, prv, slot, base, gatec, helpB, helpA = plan(cores, topo)
+    out, lands = calls(cores, topo)
+    partner, nxt, prv, slot, role = plan(cores, topo)
     S = T.sem
+    rank = T.rank_of(core)
 
-    def cnt(m):
-        return bin(m).count("1")
+    def view(e, piece):
+        a = slot[e] * NC
+        if piece == "s":
+            return T.ws[:, a:a + NC]
+        if piece == "S":
+            a = min(a, slot[partner[e]] * NC)
+            return T.ws[:, a:a + 2 * NC]
+        a += int(piece) * NH
+        return T.wc[:, a:a + NH].bitcast(dt.uint8)
 
-    def codes(a, run):
-        c0, c1 = (0, NB) if run == "B" else (NB, NC)
-        return T.wc[:, a * NC + c0:a * NC + c1].bitcast(dt.uint8)
-
-    def planes(a, k=1):
-        return T.ws[:, a * NC:(a + k) * NC]
-
-    def send(dsts, view, sem, mask):
+    have, total = [], 0
+    for e, piece, ds, m in out.get(core, []):
+        for x, p in ([(e, "s"), (partner[e], "s")] if piece == "S" else [(e, piece)]):
+            needs = [("qw%s" % h, 1) for h in ("01" if p == "s" else p)] if x == rank else [("a%d%s" % (x, p), lands.get((core, x, p)))]
+            for s, n in needs:
+                if s not in have:
+                    have.append(s)
+                    g.wait_ge(S[s], n)
         ids = []
-        for d in dsts:
+        for d in ds:
             rid, pid = topo.addr(d, core)
             ids.append(DstId(rid=rid, pnc=pid))
-        return RemoteDMATransfer(dst_ids=ids, dma_engine_mask=mask, remote_sem=sem, srcs=[view], dsts=[view] * len(ids))
-
-    def onchip(src, dst, far):
-        return topo.mask(src, dst) & ~topo.mask(src, far)
-
-    rank = T.rank_of(core)
+        v = view(e, piece)
+        g.remote_dma_fused([RemoteDMATransfer(dst_ids=ids, dma_engine_mask=m, remote_sem=S["a%d%s" % (e, piece)],
+                                              srcs=[v], dsts=[v] * len(ids))], local_sem=S.sent)
+        total += bin(m).count("1")
+    if total:
+        g.wait_ge(S.sent, total)
     if rank is None:
-        for r in range(N):
-            cr, cn, cp = cores[r], cores[nxt[r]], cores[prv[r]]
-            if core == gatec[r]:
-                a, pa = slot[partner[r]], cores[partner[r]]
-                mn, mp, mr = topo.mask(core, cn), topo.mask(core, cp), onchip(core, cr, cn)
-                g.wait_ge(S.hin, cnt(topo.mask(pa, core)))
-                g.remote_dma_fused([send([cn], codes(a, "B"), S.rnextB, mn)], local_sem=S.sent)
-                g.remote_dma_fused([send([cp], codes(a, "B"), S.rprevB, mp)], local_sem=S.sent)
-                g.remote_dma_fused([send([cr], codes(a, "B"), S.bin, mr)], local_sem=S.sent)
-                g.wait_ge(S.sent, cnt(mn) + cnt(mp) + cnt(mr))
-            for run, h in (("B", helpB[r]), ("A", helpA[r])):
-                if core == h:
-                    a = slot[r]
-                    mn, mp = topo.mask(core, cn), topo.mask(core, cp)
-                    g.wait_ge(S.hin, cnt(onchip(cr, core, cores[partner[r]])))
-                    g.remote_dma_fused([send([cp], codes(a, run), S["oprev" + run], mp)], local_sem=S.sent)
-                    g.remote_dma_fused([send([cn], codes(a, run), S["onext" + run], mn)], local_sem=S.sent)
-                    g.wait_ge(S.sent, cnt(mn) + cnt(mp))
         return
 
-    pr = partner[rank]
-    pa, pg, cn, cp = cores[pr], gatec[pr], cores[nxt[rank]], cores[prv[rank]]
-    hb, ha = helpB[rank], helpA[rank]
-    mpa, mpg, mn, mp = topo.mask(core, pa), topo.mask(core, pg), topo.mask(core, cn), topo.mask(core, cp)
-    mhb, mha = onchip(core, hb, pg), onchip(core, ha, pa)
-    both = mn & mp
-    me, po = slot[rank], slot[pr]
-
-    g.sync.dma_start(T.wt[:], T.w[:]).then_inc(S.lw, 16)
+    HB = 4 * NH
+    g.sync.dma_start(T.wt[:, 0:HB], T.w[:, 0:HB]).then_inc(S.lw0, 16)
+    g.scalar.dma_start(T.wt[:, HB:2 * HB], T.w[:, HB:2 * HB]).then_inc(S.lw1, 16)
     g.sync.dma_start(T.xt[:], T.x[:]).then_inc(S.lx, 16)
     g.sync.dma_start(T.rtt[:], T.rt[:]).then_inc(S.lr, 16)
 
-    g.wait_ge(S.qw, 1)
-    g.remote_dma_fused([send([pa], planes(me), S.pin, mpa)], local_sem=S.sent)
-    g.remote_dma_fused([send([pg], codes(me, "B"), S.hin, mpg), send([hb], codes(me, "B"), S.hin, mhb)], local_sem=S.sent)
-    g.remote_dma_fused([send([pa], codes(me, "A"), S.ain, mpa), send([ha], codes(me, "A"), S.hin, mha)], local_sem=S.sent)
-    g.wait_ge(S.pin, cnt(topo.mask(pa, core)))
-    g.remote_dma_fused([send([cn, cp], planes(base[rank], 2), S["pl%d" % rank], both)], local_sem=S.sent)
-    g.wait_ge(S.ain, cnt(topo.mask(pa, core)))
-    g.remote_dma_fused([send([cn], codes(po, "A"), S.rnextA, mn)], local_sem=S.sent)
-    g.remote_dma_fused([send([cp], codes(po, "A"), S.rprevA, mp)], local_sem=S.sent)
-    g.wait_ge(S.sent, 2 * cnt(mpa) + cnt(mpg) + cnt(mhb) + cnt(mha) + cnt(both) + cnt(mn) + cnt(mp))
-
-    up, dn = prv[rank], nxt[rank]
-    cu, cd = cores[up], cores[dn]
-    pu = cnt(topo.mask(cu, core) & topo.mask(cu, cores[prv[up]]))
-    pd = cnt(topo.mask(cd, core) & topo.mask(cd, cores[nxt[dn]]))
-    tiles = [
-        (rank, []),
-        (pr, [(S.pin, cnt(topo.mask(pa, core))), (S.ain, cnt(topo.mask(pa, core))),
-              (S.bin, cnt(onchip(gatec[rank], core, cn)))]),
-        (dn, [(S["pl%d" % dn], pd), (S.oprevB, cnt(topo.mask(helpB[dn], core))), (S.oprevA, cnt(topo.mask(helpA[dn], core)))]),
-        (partner[up], [(S["pl%d" % up], pu), (S.rnextB, cnt(topo.mask(gatec[up], core))), (S.rnextA, cnt(topo.mask(cu, core)))]),
-        (up, [(S.onextB, cnt(topo.mask(helpB[up], core))), (S.onextA, cnt(topo.mask(helpA[up], core)))]),
-        (partner[dn], [(S.rprevB, cnt(topo.mask(gatec[dn], core))), (S.rprevA, cnt(topo.mask(cd, core)))]),
-    ]
-
     v = g.vector
-    v.wait_ge(S.lw, 16)
-    v.quantize_mx(T.wc[:, me * NC:(me + 1) * NC], T.ws[:, me * NC:(me + 1) * NC], T.wt[:]).then_inc(S.qw, 1)
+    for h in range(2):
+        a = slot[rank] * NC + h * NH
+        v.wait_ge(S["lw%d" % h], 16)
+        v.quantize_mx(T.wc[:, a:a + NH], T.ws[:, a:a + NH], T.wt[:, h * HB:(h + 1) * HB]).then_inc(S["qw%d" % h], 1)
     v.wait_ge(S.lx, 16)
     v.quantize_mx(T.xc[:], T.xs[:], T.xt[:]).then_inc(S.qx, 1)
     v.wait_ge(S.lr, 16)
     v.quantize_mx(T.rc[:], T.rs[:], T.rtt[:]).then_inc(S.qx, 1)
 
+    who = {"own": rank, "par": partner[rank], "nx": nxt[rank], "pv": prv[rank],
+           "nxpar": partner[nxt[rank]], "pvpar": partner[prv[rank]]}
     t = g.tensor
     t.wait_ge(S.qx, 2)
     t.matmul_mx(T.ps[:, 0:128], T.xc[:], T.xs[:], T.rc[:], T.rs[:], True, True).then_inc(S.mm, 1)
-    t.wait_ge(S.qw, 1)
-    parts = []
-    for i, (e, waits) in enumerate(tiles):
-        for s, n in waits:
-            t.wait_ge(s, n)
-        pieces = [(0, NC)] if i + 1 < N else [(0, NC // 2), (NC // 2, NC // 2)]
-        for c0, w in pieces:
-            b = 1 + len(parts)
+    parts, have = [], []
+    for i, (o, halves) in enumerate(ORDER):
+        e = who[o]
+        for c0, w in ([(0, NH), (NH, NH)] if halves else [(0, NC)]):
+            needs = []
+            for p in ["s"] + [str(h) for h in range(c0 // NH, (c0 + w) // NH)]:
+                if e == rank:
+                    needs += [("qw%s" % h, 1) for h in ("01" if p == "s" else p)]
+                elif (core, e, p) in lands:
+                    needs.append(("a%d%s" % (e, p), lands[core, e, p]))
+                else:
+                    x = e if (core, e, "S") in lands else partner[e]
+                    needs.append(("a%dS" % x, lands[core, x, "S"]))
+            for s, n in needs:
+                if s not in have:
+                    have.append(s)
+                    t.wait_ge(S[s], n)
+            k = len(parts)
+            b = 1 + k % 7
+            if k >= 7:
+                t.wait_ge(S.zs, k - 6)
             a = slot[e] * NC + c0
             t.matmul_mx(T.ps[:, b * BANK:b * BANK + w], T.xc[:], T.xs[:], T.wc[:, a:a + w], T.ws[:, a:a + w],
                         True, True).then_inc(S.mm, 1)
@@ -190,15 +197,24 @@ def rank_program(g, core, T, topo):
                             ActivationFunctionType.Copy, scale=T.gate[:, e:e + 1]).then_inc(S.zs, 1)
 
     done = 0
+    last = {0: 0, NH: 0}
     for k, (e, c0, w, b, i) in enumerate(parts):
         if i == 0:
             continue
         v.wait_ge(S.zs, k + 1)
-        if done and (i + 1 < N or c0 == 0):
-            v.wait_ge(S.av, done)
+        mine = [c for c in last if c0 <= c < c0 + w]
+        need = max(last[c] for c in mine)
+        if need:
+            v.wait_ge(S.av, need)
         prev = T.z[:, c0:c0 + w] if i == 1 else T.acc[:, c0:c0 + w]
         v.tensor_tensor(T.acc[:, c0:c0 + w], prev, T.z[:, i * NC + c0:i * NC + c0 + w], AluOpType.add).then_inc(S.av, 1)
         done += 1
-    g.sync.wait_ge(S.av, done)
-    g.sync.dma_start(T.y[:], T.acc[:]).then_inc(S.st, 16)
-    g.sync.wait_ge(S.st, 16)
+        for c in mine:
+            last[c] = done
+
+    g.sync.wait_ge(S.av, last[0])
+    g.sync.dma_start(T.y[:, 0:NH], T.acc[:, 0:NH]).then_inc(S.st0, 16)
+    g.scalar.wait_ge(S.av, last[NH])
+    g.scalar.dma_start(T.y[:, NH:NC], T.acc[:, NH:NC]).then_inc(S.st1, 16)
+    g.sync.wait_ge(S.st0, 16)
+    g.scalar.wait_ge(S.st1, 16)

from concourse.bass import DstId, RemoteDMATransfer
from concourse.mybir import dt, AluOpType, AxisListType, ActivationFunctionType

N = 6
NC = 256
NH = 128
NT = 128
BANK = 512
FAR = -1e29

SCHED = {
    "R": [("own", "0", ["pK"]), ("own", "s", ["pR"]), ("own", "0", ["G"]), ("own", "1", ["pR"]), ("own", "1", ["H"]),
          ("own", "S", ["p", "n"]), ("par", "1", ["n"]), ("par", "1", ["p"])],
    "G": [("own", "0", ["p"]), ("own", "0", ["n"])],
    "H": [("own", "1", ["p"]), ("own", "1", ["n"])],
    "K": [("par", "0", ["n"]), ("par", "0", ["p"]), ("par", "0", ["R"])],
}
ORDER = [("own", False), ("par", False), ("nx", True), ("pvpar", True), ("pv", True), ("nxpar", True)]

SCRATCH = {
    "wt": ("sbuf", [128, 4 * NC], "bfloat16"),
    "xt": ("sbuf", [128, 4 * NT], "bfloat16"),
    "rtt": ("sbuf", [128, 512], "bfloat16"),
    "wc": ("sbuf", [128, N * NC], "float8_e4m3fn_x4"),
    "ws": ("sbuf", [128, N * NC], "uint8"),
    "xc": ("sbuf", [128, NT], "float8_e4m3fn_x4"),
    "xs": ("sbuf", [128, NT], "uint8"),
    "rc": ("sbuf", [128, 128], "float8_e4m3fn_x4"),
    "rs": ("sbuf", [128, 128], "uint8"),
    "m1": ("sbuf", [128, 4], "float32"),
    "m2": ("sbuf", [128, 4], "float32"),
    "ta": ("sbuf", [128, 8], "float32"),
    "tb": ("sbuf", [128, 8], "float32"),
    "tc": ("sbuf", [128, 8], "float32"),
    "gate": ("sbuf", [128, 8], "float32"),
    "z": ("sbuf", [128, N * NC], "float32"),
    "acc": ("sbuf", [128, NC], "float32"),
    "ps": ("psum", [128, 8 * BANK], "float32"),
}
SEMAPHORES = (["lw0", "lw1", "lx", "lr", "qw0", "qw1", "qx", "mm", "rv", "gt", "zs", "av", "st0", "st1", "sent"]
              + ["a%d%s" % (e, p) for e in range(N) for p in "01sS"])


def plan(cores, topo):
    n = len(cores)
    rk = [topo.rack(topo.host(c)) for c in cores]
    partner, nxt, prv = {}, {}, {}
    for r, c in enumerate(cores):
        partner[r] = [s for s, d in enumerate(cores) if rk[s] != rk[r] and topo.chip(d) == topo.chip(c)
                      and topo.may_write(c, d)][0]
    for rack in sorted(set(rk)):
        ring = sorted([r for r in range(n) if rk[r] == rack], key=lambda r: min(r, partner[r]))
        for i, r in enumerate(ring):
            nxt[r], prv[r] = ring[(i + 1) % len(ring)], ring[i - 1]
    order = []
    for r in range(n):
        if r not in order:
            order += [r, partner[r]]
    slot = {r: order.index(r) for r in range(n)}
    role = {}
    for r, c in enumerate(cores):
        first = c - c % 8
        near = [h for h in range(first, first + 8) if h != c
                and topo.may_write(h, cores[prv[r]]) and topo.may_write(h, cores[nxt[r]])]
        near.sort(key=lambda h: topo.die(h) != topo.die(c))
        role[r] = {"R": c, "G": near[0], "H": near[-2], "K": near[-1]}
    return partner, nxt, prv, slot, role


def calls(cores, topo):
    partner, nxt, prv, slot, role = plan(cores, topo)
    out, lands = {}, {}
    for r in range(len(cores)):
        tile = {"own": r, "par": partner[r]}
        place = dict(role[r])
        place.update({"n": cores[nxt[r]], "p": cores[prv[r]]})
        for k, c in role[partner[r]].items():
            place["p" + k] = c
        for k, rows in SCHED.items():
            src = role[r][k]
            for t, piece, dst in rows:
                ds = [place[d] for d in dst]
                m = topo.mask(src, ds[0])
                for d in ds[1:]:
                    m &= topo.mask(src, d)
                if dst[0] in role[r]:
                    m &= ~topo.mask(src, place["n"])
                out.setdefault(src, []).append((tile[t], piece, ds, m))
                for d in ds:
                    lands[d, tile[t], piece] = bin(m).count("1")
    return out, lands


def rank_program(g, core, T, topo):
    cores = list(T.cores)
    out, lands = calls(cores, topo)
    partner, nxt, prv, slot, role = plan(cores, topo)
    S = T.sem
    rank = T.rank_of(core)

    def view(e, piece):
        a = slot[e] * NC
        if piece == "s":
            return T.ws[:, a:a + NC]
        if piece == "S":
            a = min(a, slot[partner[e]] * NC)
            return T.ws[:, a:a + 2 * NC]
        a += int(piece) * NH
        return T.wc[:, a:a + NH].bitcast(dt.uint8)

    have, total = [], 0
    for e, piece, ds, m in out.get(core, []):
        for x, p in ([(e, "s"), (partner[e], "s")] if piece == "S" else [(e, piece)]):
            needs = [("qw%s" % h, 1) for h in ("01" if p == "s" else p)] if x == rank else [("a%d%s" % (x, p), lands.get((core, x, p)))]
            for s, n in needs:
                if s not in have:
                    have.append(s)
                    g.wait_ge(S[s], n)
        ids = []
        for d in ds:
            rid, pid = topo.addr(d, core)
            ids.append(DstId(rid=rid, pnc=pid))
        v = view(e, piece)
        g.remote_dma_fused([RemoteDMATransfer(dst_ids=ids, dma_engine_mask=m, remote_sem=S["a%d%s" % (e, piece)],
                                              srcs=[v], dsts=[v] * len(ids))], local_sem=S.sent)
        total += bin(m).count("1")
    if total:
        g.wait_ge(S.sent, total)
    if rank is None:
        return

    HB = 4 * NH
    g.sync.dma_start(T.wt[:, 0:HB], T.w[:, 0:HB]).then_inc(S.lw0, 16)
    g.scalar.dma_start(T.wt[:, HB:2 * HB], T.w[:, HB:2 * HB]).then_inc(S.lw1, 16)
    g.sync.dma_start(T.xt[:], T.x[:]).then_inc(S.lx, 16)
    g.sync.dma_start(T.rtt[:], T.rt[:]).then_inc(S.lr, 16)

    v = g.vector
    for h in range(2):
        a = slot[rank] * NC + h * NH
        v.wait_ge(S["lw%d" % h], 16)
        v.quantize_mx(T.wc[:, a:a + NH], T.ws[:, a:a + NH], T.wt[:, h * HB:(h + 1) * HB]).then_inc(S["qw%d" % h], 1)
    v.wait_ge(S.lx, 16)
    v.quantize_mx(T.xc[:], T.xs[:], T.xt[:]).then_inc(S.qx, 1)
    v.wait_ge(S.lr, 16)
    v.quantize_mx(T.rc[:], T.rs[:], T.rtt[:]).then_inc(S.qx, 1)

    who = {"own": rank, "par": partner[rank], "nx": nxt[rank], "pv": prv[rank],
           "nxpar": partner[nxt[rank]], "pvpar": partner[prv[rank]]}
    t = g.tensor
    t.wait_ge(S.qx, 2)
    t.matmul_mx(T.ps[:, 0:128], T.xc[:], T.xs[:], T.rc[:], T.rs[:], True, True).then_inc(S.mm, 1)
    parts, have = [], []
    for i, (o, halves) in enumerate(ORDER):
        e = who[o]
        for c0, w in ([(0, NH), (NH, NH)] if halves else [(0, NC)]):
            needs = []
            for p in ["s"] + [str(h) for h in range(c0 // NH, (c0 + w) // NH)]:
                if e == rank:
                    needs += [("qw%s" % h, 1) for h in ("01" if p == "s" else p)]
                elif (core, e, p) in lands:
                    needs.append(("a%d%s" % (e, p), lands[core, e, p]))
                else:
                    x = e if (core, e, "S") in lands else partner[e]
                    needs.append(("a%dS" % x, lands[core, x, "S"]))
            for s, n in needs:
                if s not in have:
                    have.append(s)
                    t.wait_ge(S[s], n)
            k = len(parts)
            b = 1 + k % 7
            if k >= 7:
                t.wait_ge(S.zs, k - 6)
            a = slot[e] * NC + c0
            t.matmul_mx(T.ps[:, b * BANK:b * BANK + w], T.xc[:], T.xs[:], T.wc[:, a:a + w], T.ws[:, a:a + w],
                        True, True).then_inc(S.mm, 1)
            parts.append((e, c0, w, b, i))

    L = T.ps[:, 0:N]
    v.wait_ge(S.mm, 1)
    v.tensor_reduce(T.m1[:, 0:1], L, AxisListType.X, AluOpType.max).then_inc(S.rv, 1)
    v.wait_ge(S.rv, 1)
    v.tensor_scalar(T.ta[:, 0:N], L, T.m1[:, 0:1], FAR, AluOpType.is_ge, AluOpType.mult).then_inc(S.rv, 1)
    v.wait_ge(S.rv, 2)
    v.tensor_tensor(T.tb[:, 0:N], L, T.ta[:, 0:N], AluOpType.add).then_inc(S.rv, 1)
    v.wait_ge(S.rv, 3)
    v.tensor_reduce(T.m2[:, 0:1], T.tb[:, 0:N], AxisListType.X, AluOpType.max).then_inc(S.rv, 1)
    v.wait_ge(S.rv, 4)
    v.tensor_scalar(T.tc[:, 0:N], L, T.m2[:, 0:1], None, AluOpType.is_ge).then_inc(S.rv, 1)
    v.wait_ge(S.rv, 5)
    v.tensor_tensor(T.gate[:, 0:N], L, T.tc[:, 0:N], AluOpType.mult).then_inc(S.gt, 1)

    g.scalar.wait_ge(S.gt, 1)
    for k, (e, c0, w, b, i) in enumerate(parts):
        g.scalar.wait_ge(S.mm, 2 + k)
        g.scalar.activation(T.z[:, i * NC + c0:i * NC + c0 + w], T.ps[:, b * BANK:b * BANK + w],
                            ActivationFunctionType.Copy, scale=T.gate[:, e:e + 1]).then_inc(S.zs, 1)

    done = 0
    last = {0: 0, NH: 0}
    for k, (e, c0, w, b, i) in enumerate(parts):
        if i == 0:
            continue
        v.wait_ge(S.zs, k + 1)
        mine = [c for c in last if c0 <= c < c0 + w]
        need = max(last[c] for c in mine)
        if need:
            v.wait_ge(S.av, need)
        prev = T.z[:, c0:c0 + w] if i == 1 else T.acc[:, c0:c0 + w]
        v.tensor_tensor(T.acc[:, c0:c0 + w], prev, T.z[:, i * NC + c0:i * NC + c0 + w], AluOpType.add).then_inc(S.av, 1)
        done += 1
        for c in mine:
            last[c] = done

    g.sync.wait_ge(S.av, last[0])
    g.sync.dma_start(T.y[:, 0:NH], T.acc[:, 0:NH]).then_inc(S.st0, 16)
    g.scalar.wait_ge(S.av, last[NH])
    g.scalar.dma_start(T.y[:, NH:NC], T.acc[:, NH:NC]).then_inc(S.st1, 16)
    g.sync.wait_ge(S.st0, 16)
    g.scalar.wait_ge(S.st1, 16)
